import numpy as np
import ml_dtypes


def mxq(x, axis, fmt="e4m3"):
    dtype, down = {"e4m3": (ml_dtypes.float8_e4m3fn, 7), "e5m2": (ml_dtypes.float8_e5m2, 14)}[fmt]
    v = np.moveaxis(np.asarray(x, np.float32).astype(ml_dtypes.bfloat16).astype(np.float64), axis, -1)
    blocks = v.reshape(v.shape[:-1] + (-1, 32))
    amax = np.abs(blocks).max(-1, keepdims=True)
    byte = np.maximum(np.where(amax > 0, np.frexp(amax)[1] - 1 + 127, 0) - down, 1)
    scale = np.exp2(byte - 127.0)
    codes = (blocks / scale).astype(np.float32).astype(dtype).astype(np.float64)
    return np.moveaxis((codes * scale).reshape(v.shape), -1, axis)


WIDE = False


def mx_kscale(k):
    if not WIDE:
        return np.ones(k)
    levels = np.array([30, -30])
    if k % 512:
        return np.exp2(np.random.permutation(np.resize(levels, k // 32))).repeat(32)
    a = np.empty((k // 512, 16))
    for p in range(k // 512):
        a[p, :8] = np.random.permutation(np.resize(levels, 8))
        for g in range(8):
            far = levels[np.abs(levels - a[p, g]) >= 10]
            a[p, g + 8] = far[np.random.randint(len(far))]
    return np.exp2(a.ravel()).repeat(32)


def f64(x):
    return np.asarray(x).astype(np.float64)


def striped(idx):
    return np.tile(np.asarray(idx).reshape(-1, 16).T, (8, 1)).astype(np.uint16)


def unstriped(offs):
    return offs[:16].T.reshape(-1).astype(np.int64)


E2M1 = np.array([0.0, 0.5, 1.0, 1.5, 2.0, 3.0, 4.0, 6.0, -0.0, -0.5, -1.0, -1.5, -2.0, -3.0, -4.0, -6.0])


def pack_weight(w, fmt):
    k, n = w.shape
    w = f64(np.asarray(w, np.float32).astype(ml_dtypes.bfloat16)).reshape(k // 32, 32, n)
    amax = np.abs(w).max(1)
    if fmt == "e4m3":
        byte = np.frexp(amax)[1] - 1 + 127 - 7
    else:
        mant, ex = np.frexp(amax / 6.0)
        byte = np.where(mant > 0.5, ex, ex - 1) + 127
    byte = np.clip(np.where(amax > 0, byte, 1), 1, 254)
    scaled = (w * np.exp2(127.0 - byte)[:, None, :]).reshape(k, n).astype(np.float32)
    by_word = np.ascontiguousarray(scaled.reshape(k // 512, 128, 4, n).transpose(0, 1, 3, 2))
    if fmt == "e4m3":
        words = by_word.astype(ml_dtypes.float8_e4m3fn).view(np.uint8)
    else:
        c = by_word.astype(ml_dtypes.float4_e2m1fn).view(np.uint8) & 0xF
        words = (c[..., 0::2] | (c[..., 1::2] << 4)).reshape(k // 512, 128, 2 * n)
    return np.ascontiguousarray(words), np.ascontiguousarray(byte.astype(np.uint8).reshape(k // 512, 16, n))


def unpack_weight(words, scales, fmt):
    g, _, n = scales.shape
    words = np.ascontiguousarray(words).reshape(g, 128, n, -1)
    if fmt == "e4m3":
        vals = words.view(ml_dtypes.float8_e4m3fn).astype(np.float64)
    else:
        nib = np.empty((g, 128, n, 4), np.uint8)
        nib[..., 0::2] = words & 0xF
        nib[..., 1::2] = words >> 4
        vals = E2M1[nib]
    vals = vals * np.repeat(np.exp2(scales.astype(np.float64) - 127.0), 8, axis=1)[..., None]
    return vals.transpose(0, 1, 3, 2).reshape(g * 512, n)


K, T, J, I, L, S, R, F, Z, N = 512, 512, 256, 128, 128, 512, 512, 512, 1024, 256


def setup_inputs():
    n = np.random.standard_normal
    idx = np.random.permutation(T)[:I]
    idx2 = np.random.permutation(S)[:L]
    idx3 = np.random.permutation(Z)[:J]
    fk = mx_kscale(K)
    fr = mx_kscale(R)
    ff = mx_kscale(F)
    wp = pack_weight(n((K, R)) * 1 / np.sqrt(K) * fk[:, None] * fr, "e2m1")
    w2p = pack_weight(n((F, R)) * 1 / np.sqrt(F) * ff[:, None] * fr, "e2m1")
    wbp = pack_weight(n((R, N)) * 1 / np.sqrt(R) / fr[:, None], "e2m1")
    return {
        "xa": (n((K, T)) / fk[:, None]).astype(np.float32),
        "xb": (n((K, S)) * 0.6 / fk[:, None]).astype(np.float32),
        "w_words": wp[0],
        "w_scales": wp[1],
        "xo": (n((F, Z))).astype(np.float32),
        "fl": (np.random.uniform(0.5, 2.0, (F, 1)) / ff[:, None]).astype(np.float32),
        "so": (n((F, J)) * 0.8).astype(np.float32),
        "w2_words": w2p[0],
        "w2_scales": w2p[1],
        "wb_words": wbp[0],
        "wb_scales": wbp[1],
        "rs": (1.0 * n((J, N))).astype(np.float32),
        "offs": striped(idx),
        "offs2": striped(idx2),
        "offs3": striped(idx3),
    }


def reference(xa, xb, w_words, w_scales, xo, fl, so, w2_words, w2_scales, wb_words, wb_scales, rs, offs, offs2, offs3):
    idx = unstriped(offs)
    idx2 = unstriped(offs2)
    idx3 = unstriped(offs3)
    wu = unpack_weight(w_words, w_scales, "e2m1")
    w2u = unpack_weight(w2_words, w2_scales, "e2m1")
    wbu = unpack_weight(wb_words, wb_scales, "e2m1")
    u = np.concatenate([f64(xa)[:, idx], f64(xb)[:, idx2]], axis=1)
    u2 = np.maximum(f64(xo)[:, idx3], f64(so)) * f64(fl)
    uq = mxq(u, 0, "e4m3")
    a = wu.T @ uq
    u2q = mxq(u2, 0, "e5m2")
    q = w2u.T @ u2q
    hid = np.abs(a - q)
    hidq = mxq(hid, 0, "e5m2")
    p = hidq.T @ wbu
    pk2 = np.max(np.abs(p), axis=1, keepdims=True)
    y = p / (pk2 + 0.2) + 0.3 * f64(rs)
    return y

@@ -1,0 +1,197 @@
+from contextlib import ExitStack
+
+import concourse.mybir as mybir
+
+F32 = mybir.dt.float32
+BF16 = mybir.dt.bfloat16
+I32 = mybir.dt.int32
+U32 = mybir.dt.uint32
+U16 = mybir.dt.uint16
+U8 = mybir.dt.uint8
+E4M3 = mybir.dt.float8_e4m3fn_x4
+E5M2 = mybir.dt.float8_e5m2_x4
+E2M1 = mybir.dt.float4_e2m1fn_x4
+ALU = mybir.AluOpType
+ACT = mybir.ActivationFunctionType
+
+P = 128
+PACK = 4
+T = 512
+Z = 1024
+J = 256
+H = 128
+R = 512
+N = 256
+FLOPS = 2 * 512 * R * J * 2 + 2 * R * J * N
+
+
+def tile_list_two_joined_largest_absgap_rowpeaks_kernel(
+    tc, xa, xb, w_words, w_scales, xo, fl, so, w2_words, w2_scales, wb_words, wb_scales, rs, offs, offs2, offs3, out
+):
+    nc = tc.nc
+    with ExitStack() as ctx:
+        keep = ctx.enter_context(tc.tile_pool(name="keep", bufs=1))
+        psum = ctx.enter_context(tc.psum_pool(name="psum", bufs=1))
+
+        def sb(name, shape, dtype):
+            return keep.tile(shape, dtype, name=name, align_bytes=64)
+
+        def load_words(engine, name, words):
+            tile = sb(name, [P, words.shape[2]], U8)
+            engine.dma_start(out=tile[:].bitcast(I32), in_=words[0].bitcast(I32))
+            return tile
+
+        def load_scales(engine, name, scales):
+            tile = sb(name, [P, scales.shape[2] // 4], I32)
+            for q in range(4):
+                rows = scales[0, 4 * q : 4 * q + 4, :].bitcast(I32)
+                engine.dma_start(
+                    out=tile[32 * q : 32 * (q + 1), :], in_=rows.unsqueeze(0).broadcast_to([8, 4, rows.shape[1]])
+                )
+            return tile[:].bitcast(U8)
+
+        def load_planes(name, table, first, count):
+            width = table.shape[1]
+            rows = table.rearrange("(p t) c -> p (t c)", t=PACK)
+            tile = sb("%s%d" % (name, first), [P, count * width], F32)
+            nc.sync.dma_start(out=tile[:], in_=rows[:, first * width : (first + count) * width])
+            return [tile[:, i * width : (i + 1) * width] for i in range(count)]
+
+        list_o = keep.tile([P, J // 16], U16, name="list_o")
+        list_a = keep.tile([P, H // 16], U16, name="list_a")
+        list_b = keep.tile([P, H // 16], U16, name="list_b")
+
+        fl_sb = sb("fl_sb", [P, PACK], F32)
+        nc.gpsimd.dma_start(out=fl_sb[:], in_=fl.rearrange("(p t) o -> p (t o)", t=PACK))
+        wb_sb = load_words(nc.gpsimd, "wb_sb", wb_words)
+        wbs_sb = load_scales(nc.gpsimd, "wbs_sb", wb_scales)
+
+        nc.sync.dma_start(list_o[:], offs3)
+        w2_raw = load_words(nc.sync, "w2_raw", w2_words)
+        w2s_raw = load_scales(nc.sync, "w2s_raw", w2_scales)
+        so_win = load_planes("so", so, 0, PACK)
+        xo_win = load_planes("xo", xo, 0, 1)
+        w_raw = load_words(nc.sync, "w_raw", w_words)
+        xo_win = xo_win + load_planes("xo", xo, 1, 1)
+        ws_raw = load_scales(nc.sync, "ws_raw", w_scales)
+        xo_win = xo_win + load_planes("xo", xo, 2, 1) + load_planes("xo", xo, 3, 1)
+        xa_win = load_planes("xa", xa, 0, 2)
+        nc.sync.dma_start(list_a[:], offs)
+        xa_win = xa_win + load_planes("xa", xa, 2, 2)
+        nc.sync.dma_start(list_b[:], offs2)
+        xb_win = load_planes("xb", xb, 0, 2) + load_planes("xb", xb, 2, 1) + load_planes("xb", xb, 3, 1)
+        rs_sb = sb("rs_sb", [P, 2, N], F32)
+        nc.sync.dma_start(out=rs_sb[:], in_=rs.rearrange("(h p) n -> p h n", h=2))
+
+        neg_fl = sb("neg_fl", [P, PACK], F32)
+        nc.scalar.activation(out=neg_fl[:], in_=fl_sb[:], func=ACT.Copy, scale=-1.0)
+
+        def deal_words(copy, name, words):
+            dealt = sb(name, [P, 2 * R], U8)
+            copy(
+                out=dealt[:].bitcast(U16).rearrange("p (t m) -> p t m", t=PACK),
+                in_=words[:].bitcast(U16).rearrange("p (m t) -> p t m", t=PACK),
+            )
+            return dealt
+
+        def deal_scales(name, scales):
+            dealt = sb(name, [P, R], U8)
+            nc.vector.tensor_copy(
+                out=dealt[:].rearrange("p (t m) -> p t m", t=PACK), in_=scales.rearrange("p (m t) -> p t m", t=PACK)
+            )
+            return dealt
+
+        w2_d = deal_words(nc.vector.tensor_copy, "w2_d", w2_raw)
+        w2s_d = deal_scales("w2s_d", w2s_raw)
+
+        def quantize(name, grouped, cols, fmt):
+            codes = sb(name + "_codes", [P, cols], U32)
+            scales = sb(name + "_scales", [P, cols], U8)
+            nc.vector.quantize_mx(
+                out=codes[:].bitcast(fmt), scales=scales[:], in_=grouped[:].rearrange("p j t -> p (j t)")
+            )
+            return codes, scales
+
+        u2 = sb("u2", [P, J, PACK], BF16)
+        for t in range(PACK):
+            picked = sb("picked%d" % t, [P, J], F32)
+            nc.scalar.activation(out=picked[:], in_=xo_win[t].indirect(list_o[:]), func=ACT.Copy)
+            larger = sb("larger%d" % t, [P, J], F32)
+            nc.vector.tensor_tensor(out=larger[:], in0=picked[:], in1=so_win[t], op=ALU.max)
+            nc.vector.tensor_scalar(
+                out=u2[:, :, t], in0=larger[:], scalar1=neg_fl[:, t : t + 1], scalar2=None, op0=ALU.mult
+            )
+        w_d = deal_words(nc.scalar.copy, "w_d", w_raw)
+        ws_d = deal_scales("ws_d", ws_raw)
+        u2_codes, u2_scales = quantize("u2", u2, J, E5M2)
+
+        gap = [psum.tile([P, PACK * H], F32, name="gap%d" % h) for h in range(2)]
+        prod = [psum.tile([P, N], F32, name="prod%d" % h) for h in range(2)]
+
+        def first_stage(h, words, scales, codes, code_scales, fmt, start, stop):
+            for t in range(PACK):
+                nc.tensor.matmul_mx(
+                    out=gap[h][:, t * H : (t + 1) * H],
+                    lhsT=words[:, 2 * t * P : 2 * (t + 1) * P].bitcast(E2M1),
+                    lhsT_scale=scales[:, t * P : (t + 1) * P],
+                    rhs=codes.bitcast(fmt),
+                    rhs_scale=code_scales,
+                    start=start and t == 0,
+                    stop=stop and t == PACK - 1,
+                )
+
+        for h in range(2):
+            cols = slice(h * H, (h + 1) * H)
+            first_stage(h, w2_d, w2s_d, u2_codes[:, cols], u2_scales[:, cols], E5M2, True, False)
+
+        def gather_u(h, windows, lst):
+            u = sb("u", [P, H, PACK], BF16)
+            for t in range(PACK):
+                nc.vector.tensor_copy(out=u[:, :, t], in_=windows[t].indirect(lst[:]))
+            return u
+
+        def close_gap(h, u):
+            codes, scales = quantize("u%d" % h, u, H, E4M3)
+            first_stage(h, w_d, ws_d, codes[:], scales[:], E4M3, False, True)
+            hid = sb("hid%d" % h, [P, H, PACK], BF16)
+            nc.scalar.activation(out=hid[:], in_=gap[h][:].rearrange("p (t j) -> p j t", t=PACK), func=ACT.Abs)
+            return hid
+
+        def second_stage(h, codes, scales):
+            nc.tensor.matmul_mx(
+                out=prod[h][:],
+                lhsT=codes[:].bitcast(E5M2),
+                lhsT_scale=scales[:],
+                rhs=wb_sb[:].bitcast(E2M1),
+                rhs_scale=wbs_sb,
+                start=True,
+                stop=True,
+            )
+
+        rs_part = sb("rs_part", [P, 2, N], F32)
+
+        def finish(h):
+            size = sb("size%d" % h, [P, N], F32)
+            nc.scalar.activation(out=size[:], in_=prod[h][:], func=ACT.Abs)
+            lifted = sb("lifted%d" % h, [P, N], F32)
+            peak = sb("peak%d" % h, [P, 1], F32)
+            nc.vector.tensor_scalar(
+                out=lifted[:], in0=size[:], scalar1=0.2, scalar2=None, op0=ALU.add, op1=ALU.max, accum_out=peak[:]
+            )
+            inverse = sb("inverse%d" % h, [P, 1], F32)
+            nc.vector.reciprocal(out=inverse[:], in_=peak[:])
+            result = sb("result%d" % h, [P, N], F32)
+            nc.vector.scalar_tensor_tensor(
+                out=result[:], in0=prod[h][:], scalar=inverse[:], in1=rs_part[:, h, :], op0=ALU.mult, op1=ALU.add
+            )
+            nc.sync.dma_start(out=out[h * H : (h + 1) * H, :], in_=result[:])
+
+        hid0 = close_gap(0, gather_u(0, xa_win, list_a))
+        u1 = gather_u(1, xb_win, list_b)
+        hid0_codes, hid0_scales = quantize("hid0", hid0, H, E5M2)
+        hid1 = close_gap(1, u1)
+        second_stage(0, hid0_codes, hid0_scales)
+        nc.scalar.activation(out=rs_part[:], in_=rs_sb[:], func=ACT.Copy, scale=0.3)
+        second_stage(1, *quantize("hid1", hid1, H, E5M2))
+        finish(0)
+        finish(1)

@@ -41,13 +41,11 @@ def tile_list_two_joined_largest_absgap_rowpeaks_kernel(
             engine.dma_start(out=tile[:].bitcast(I32), in_=words[0].bitcast(I32))
             return tile
 
-        def load_scales(engine, name, scales):
+        def load_scales(clear, name, scales):
             tile = sb(name, [P, scales.shape[2] // 4], I32)
+            clear.memset(tile[:], 0)
             for q in range(4):
-                rows = scales[0, 4 * q : 4 * q + 4, :].bitcast(I32)
-                engine.dma_start(
-                    out=tile[32 * q : 32 * (q + 1), :], in_=rows.unsqueeze(0).broadcast_to([8, 4, rows.shape[1]])
-                )
+                nc.sync.dma_start(out=tile[32 * q : 32 * q + 4, :], in_=scales[0, 4 * q : 4 * q + 4, :].bitcast(I32))
             return tile[:].bitcast(U8)
 
         def load_planes(name, table, first, count):
@@ -61,25 +59,23 @@ def tile_list_two_joined_largest_absgap_rowpeaks_kernel(
         list_a = keep.tile([P, H // 16], U16, name="list_a")
         list_b = keep.tile([P, H // 16], U16, name="list_b")
 
-        fl_sb = sb("fl_sb", [P, PACK], F32)
-        nc.gpsimd.dma_start(out=fl_sb[:], in_=fl.rearrange("(p t) o -> p (t o)", t=PACK))
-        wb_sb = load_words(nc.gpsimd, "wb_sb", wb_words)
-        wbs_sb = load_scales(nc.gpsimd, "wbs_sb", wb_scales)
-
         nc.sync.dma_start(list_o[:], offs3)
-        w2_raw = load_words(nc.sync, "w2_raw", w2_words)
-        w2s_raw = load_scales(nc.sync, "w2s_raw", w2_scales)
+        fl_sb = sb("fl_sb", [P, PACK], F32)
+        nc.sync.dma_start(out=fl_sb[:], in_=fl.rearrange("(p t) o -> p (t o)", t=PACK))
         so_win = load_planes("so", so, 0, PACK)
-        xo_win = load_planes("xo", xo, 0, 1)
+        xo_win = load_planes("xo", xo, 0, 1) + load_planes("xo", xo, 1, 1)
+        w2_raw = load_words(nc.sync, "w2_raw", w2_words)
         w_raw = load_words(nc.sync, "w_raw", w_words)
-        xo_win = xo_win + load_planes("xo", xo, 1, 1)
-        ws_raw = load_scales(nc.sync, "ws_raw", w_scales)
+        w2s_raw = load_scales(nc.gpsimd, "w2s_raw", w2_scales)
         xo_win = xo_win + load_planes("xo", xo, 2, 1) + load_planes("xo", xo, 3, 1)
+        ws_raw = load_scales(nc.vector, "ws_raw", w_scales)
         xa_win = load_planes("xa", xa, 0, 2)
         nc.sync.dma_start(list_a[:], offs)
         xa_win = xa_win + load_planes("xa", xa, 2, 2)
         nc.sync.dma_start(list_b[:], offs2)
         xb_win = load_planes("xb", xb, 0, 2) + load_planes("xb", xb, 2, 1) + load_planes("xb", xb, 3, 1)
+        wb_sb = load_words(nc.sync, "wb_sb", wb_words)
+        wbs_sb = load_scales(nc.vector, "wbs_sb", wb_scales)
         rs_sb = sb("rs_sb", [P, 2, N], F32)
         nc.sync.dma_start(out=rs_sb[:], in_=rs.rearrange("(h p) n -> p h n", h=2))
 
@@ -101,11 +97,9 @@ def tile_list_two_joined_largest_absgap_rowpeaks_kernel(
             )
             return dealt
 
-        w2_d = deal_words(nc.vector.tensor_copy, "w2_d", w2_raw)
-        w2s_d = deal_scales("w2s_d", w2s_raw)
 
-        def quantize(name, grouped, cols, fmt):
-            codes = sb(name + "_codes", [P, cols], U32)
+        def quantize(name, grouped, cols, fmt, codes_name=None):
+            codes = sb(codes_name or name + "_codes", [P, cols], U32)
             scales = sb(name + "_scales", [P, cols], U8)
             nc.vector.quantize_mx(
                 out=codes[:].bitcast(fmt), scales=scales[:], in_=grouped[:].rearrange("p j t -> p (j t)")
@@ -113,7 +107,8 @@ def tile_list_two_joined_largest_absgap_rowpeaks_kernel(
             return codes, scales
 
         u2 = sb("u2", [P, J, PACK], BF16)
-        for t in range(PACK):
+
+        def side_plane(t):
             picked = sb("picked%d" % t, [P, J], F32)
             nc.scalar.activation(out=picked[:], in_=xo_win[t].indirect(list_o[:]), func=ACT.Copy)
             larger = sb("larger%d" % t, [P, J], F32)
@@ -121,8 +116,15 @@ def tile_list_two_joined_largest_absgap_rowpeaks_kernel(
             nc.vector.tensor_scalar(
                 out=u2[:, :, t], in0=larger[:], scalar1=neg_fl[:, t : t + 1], scalar2=None, op0=ALU.mult
             )
-        w_d = deal_words(nc.scalar.copy, "w_d", w_raw)
+
+        side_plane(0)
+        side_plane(1)
+        w2_d = deal_words(nc.vector.tensor_copy, "w2_d", w2_raw)
+        w2s_d = deal_scales("w2s_d", w2s_raw)
+        side_plane(2)
         ws_d = deal_scales("ws_d", ws_raw)
+        side_plane(3)
+        w_d = deal_words(nc.scalar.copy, "w_d", w_raw)
         u2_codes, u2_scales = quantize("u2", u2, J, E5M2)
 
         gap = [psum.tile([P, PACK * H], F32, name="gap%d" % h) for h in range(2)]
@@ -188,9 +190,8 @@ def tile_list_two_joined_largest_absgap_rowpeaks_kernel(
 
         hid0 = close_gap(0, gather_u(0, xa_win, list_a))
         u1 = gather_u(1, xb_win, list_b)
-        hid0_codes, hid0_scales = quantize("hid0", hid0, H, E5M2)
         hid1 = close_gap(1, u1)
-        second_stage(0, hid0_codes, hid0_scales)
+        second_stage(0, *quantize("hid0", hid0, H, E5M2, "u"))
         nc.scalar.activation(out=rs_part[:], in_=rs_sb[:], func=ACT.Copy, scale=0.3)
         second_stage(1, *quantize("hid1", hid1, H, E5M2))
         finish(0)

@@ -59,10 +59,10 @@ def tile_list_two_joined_largest_absgap_rowpeaks_kernel(
         list_a = keep.tile([P, H // 16], U16, name="list_a")
         list_b = keep.tile([P, H // 16], U16, name="list_b")
 
+        so_win = load_planes("so", so, 0, PACK)
         nc.sync.dma_start(list_o[:], offs3)
         fl_sb = sb("fl_sb", [P, PACK], F32)
         nc.sync.dma_start(out=fl_sb[:], in_=fl.rearrange("(p t) o -> p (t o)", t=PACK))
-        so_win = load_planes("so", so, 0, PACK)
         xo_win = load_planes("xo", xo, 0, 1) + load_planes("xo", xo, 1, 1)
         w2_raw = load_words(nc.sync, "w2_raw", w2_words)
         w_raw = load_words(nc.sync, "w_raw", w_words)
@@ -119,12 +119,12 @@ def tile_list_two_joined_largest_absgap_rowpeaks_kernel(
 
         side_plane(0)
         side_plane(1)
+        w_d = deal_words(nc.scalar.copy, "w_d", w_raw)
         w2_d = deal_words(nc.vector.tensor_copy, "w2_d", w2_raw)
         w2s_d = deal_scales("w2s_d", w2s_raw)
         side_plane(2)
         ws_d = deal_scales("ws_d", ws_raw)
         side_plane(3)
-        w_d = deal_words(nc.scalar.copy, "w_d", w_raw)
         u2_codes, u2_scales = quantize("u2", u2, J, E5M2)
 
         gap = [psum.tile([P, PACK * H], F32, name="gap%d" % h) for h in range(2)]
@@ -146,16 +146,15 @@ def tile_list_two_joined_largest_absgap_rowpeaks_kernel(
             cols = slice(h * H, (h + 1) * H)
             first_stage(h, w2_d, w2s_d, u2_codes[:, cols], u2_scales[:, cols], E5M2, True, False)
 
-        def gather_u(h, windows, lst):
-            u = sb("u", [P, H, PACK], BF16)
-            for t in range(PACK):
-                nc.vector.tensor_copy(out=u[:, :, t], in_=windows[t].indirect(lst[:]))
-            return u
+        def pick_planes(name, windows, lst):
+            planes = sb(name, [P, len(windows), H], F32)
+            for t, window in enumerate(windows):
+                nc.scalar.activation(out=planes[:, t, :], in_=window.indirect(lst[:]), func=ACT.Copy)
+            return planes[:].rearrange("p t j -> p j t")
 
-        def close_gap(h, u):
-            codes, scales = quantize("u%d" % h, u, H, E4M3)
+        def close_gap(h, hid_name, codes, scales):
             first_stage(h, w_d, ws_d, codes[:], scales[:], E4M3, False, True)
-            hid = sb("hid%d" % h, [P, H, PACK], BF16)
+            hid = sb(hid_name, [P, H, PACK], BF16)
             nc.scalar.activation(out=hid[:], in_=gap[h][:].rearrange("p (t j) -> p j t", t=PACK), func=ACT.Abs)
             return hid
 
@@ -170,9 +169,7 @@ def tile_list_two_joined_largest_absgap_rowpeaks_kernel(
                 stop=True,
             )
 
-        rs_part = sb("rs_part", [P, 2, N], F32)
-
-        def finish(h):
+        def finish(h, rs_part):
             size = sb("size%d" % h, [P, N], F32)
             nc.scalar.activation(out=size[:], in_=prod[h][:], func=ACT.Abs)
             lifted = sb("lifted%d" % h, [P, N], F32)
@@ -188,11 +185,19 @@ def tile_list_two_joined_largest_absgap_rowpeaks_kernel(
             )
             nc.sync.dma_start(out=out[h * H : (h + 1) * H, :], in_=result[:])
 
-        hid0 = close_gap(0, gather_u(0, xa_win, list_a))
-        u1 = gather_u(1, xb_win, list_b)
-        hid1 = close_gap(1, u1)
-        second_stage(0, *quantize("hid0", hid0, H, E5M2, "u"))
-        nc.scalar.activation(out=rs_part[:], in_=rs_sb[:], func=ACT.Copy, scale=0.3)
+        u0 = sb("u0", [P, H, PACK], BF16)
+        nc.vector.tensor_copy(out=u0[:], in_=pick_planes("xa_picked", xa_win, list_a))
+        xb_picked = pick_planes("xb_picked", xb_win[0:2], list_b)
+        u0_quantized = quantize("u0", u0, H, E4M3)
+        u1 = sb("u1", [P, H, PACK], BF16)
+        nc.scalar.copy(out=u1[:, :, 0:2], in_=xb_picked)
+        hid0 = close_gap(0, "xb_picked", *u0_quantized)
+        for t in range(2, PACK):
+            nc.vector.tensor_copy(out=u1[:, :, t], in_=xb_win[t].indirect(list_b[:]))
+        hid1 = close_gap(1, "hid1", *quantize("u1", u1, H, E4M3))
+        second_stage(0, *quantize("hid0", hid0, H, E5M2, "u1"))
+        rs_part = sb("xb_picked", [P, 2, N], F32)
+        nc.vector.tensor_scalar(out=rs_part[:], in0=rs_sb[:], scalar1=0.3, scalar2=None, op0=ALU.mult)
         second_stage(1, *quantize("hid1", hid1, H, E5M2))
-        finish(0)
-        finish(1)
+        finish(0, rs_part)
+        finish(1, rs_part)

@@ -120,12 +120,12 @@ def tile_list_two_joined_largest_absgap_rowpeaks_kernel(
         side_plane(0)
         side_plane(1)
         w_d = deal_words(nc.scalar.copy, "w_d", w_raw)
-        w2_d = deal_words(nc.vector.tensor_copy, "w2_d", w2_raw)
+        w2_d = deal_words(nc.scalar.copy, "w2_d", w2_raw)
         w2s_d = deal_scales("w2s_d", w2s_raw)
         side_plane(2)
-        ws_d = deal_scales("ws_d", ws_raw)
         side_plane(3)
         u2_codes, u2_scales = quantize("u2", u2, J, E5M2)
+        ws_d = deal_scales("u2", ws_raw)
 
         gap = [psum.tile([P, PACK * H], F32, name="gap%d" % h) for h in range(2)]
         prod = [psum.tile([P, N], F32, name="prod%d" % h) for h in range(2)]
@@ -169,7 +169,7 @@ def tile_list_two_joined_largest_absgap_rowpeaks_kernel(
                 stop=True,
             )
 
-        def finish(h, rs_part):
+        def row_factor(h):
             size = sb("size%d" % h, [P, N], F32)
             nc.scalar.activation(out=size[:], in_=prod[h][:], func=ACT.Abs)
             lifted = sb("lifted%d" % h, [P, N], F32)
@@ -179,7 +179,10 @@ def tile_list_two_joined_largest_absgap_rowpeaks_kernel(
             )
             inverse = sb("inverse%d" % h, [P, 1], F32)
             nc.vector.reciprocal(out=inverse[:], in_=peak[:])
-            result = sb("result%d" % h, [P, N], F32)
+            return inverse
+
+        def finish(h, name, inverse, rs_part):
+            result = sb(name, [P, N], F32)
             nc.vector.scalar_tensor_tensor(
                 out=result[:], in0=prod[h][:], scalar=inverse[:], in1=rs_part[:, h, :], op0=ALU.mult, op1=ALU.add
             )
@@ -199,5 +202,7 @@ def tile_list_two_joined_largest_absgap_rowpeaks_kernel(
         rs_part = sb("xb_picked", [P, 2, N], F32)
         nc.vector.tensor_scalar(out=rs_part[:], in0=rs_sb[:], scalar1=0.3, scalar2=None, op0=ALU.mult)
         second_stage(1, *quantize("hid1", hid1, H, E5M2))
-        finish(0, rs_part)
-        finish(1, rs_part)
+        inverse0 = row_factor(0)
+        inverse1 = row_factor(1)
+        finish(0, "size1", inverse0, rs_part)
+        finish(1, "result1", inverse1, rs_part)

from contextlib import ExitStack

import concourse.mybir as mybir

F32 = mybir.dt.float32
BF16 = mybir.dt.bfloat16
I32 = mybir.dt.int32
U32 = mybir.dt.uint32
U16 = mybir.dt.uint16
U8 = mybir.dt.uint8
E4M3 = mybir.dt.float8_e4m3fn_x4
E5M2 = mybir.dt.float8_e5m2_x4
E2M1 = mybir.dt.float4_e2m1fn_x4
ALU = mybir.AluOpType
ACT = mybir.ActivationFunctionType

P = 128
PACK = 4
T = 512
Z = 1024
J = 256
H = 128
R = 512
N = 256
FLOPS = 2 * 512 * R * J * 2 + 2 * R * J * N


def tile_list_two_joined_largest_absgap_rowpeaks_kernel(
    tc, xa, xb, w_words, w_scales, xo, fl, so, w2_words, w2_scales, wb_words, wb_scales, rs, offs, offs2, offs3, out
):
    nc = tc.nc
    with ExitStack() as ctx:
        keep = ctx.enter_context(tc.tile_pool(name="keep", bufs=1))
        psum = ctx.enter_context(tc.psum_pool(name="psum", bufs=1))

        def sb(name, shape, dtype):
            return keep.tile(shape, dtype, name=name, align_bytes=64)

        def load_words(engine, name, words):
            tile = sb(name, [P, words.shape[2]], U8)
            engine.dma_start(out=tile[:].bitcast(I32), in_=words[0].bitcast(I32))
            return tile

        def load_scales(clear, name, scales):
            tile = sb(name, [P, scales.shape[2] // 4], I32)
            clear.memset(tile[:], 0)
            for q in range(4):
                nc.sync.dma_start(out=tile[32 * q : 32 * q + 4, :], in_=scales[0, 4 * q : 4 * q + 4, :].bitcast(I32))
            return tile[:].bitcast(U8)

        def load_planes(name, table, first, count):
            width = table.shape[1]
            rows = table.rearrange("(p t) c -> p (t c)", t=PACK)
            tile = sb("%s%d" % (name, first), [P, count * width], F32)
            nc.sync.dma_start(out=tile[:], in_=rows[:, first * width : (first + count) * width])
            return [tile[:, i * width : (i + 1) * width] for i in range(count)]

        list_o = keep.tile([P, J // 16], U16, name="list_o")
        list_a = keep.tile([P, H // 16], U16, name="list_a")
        list_b = keep.tile([P, H // 16], U16, name="list_b")

        so_win = load_planes("so", so, 0, PACK)
        nc.sync.dma_start(list_o[:], offs3)
        fl_sb = sb("fl_sb", [P, PACK], F32)
        nc.sync.dma_start(out=fl_sb[:], in_=fl.rearrange("(p t) o -> p (t o)", t=PACK))
        xo_win = load_planes("xo", xo, 0, 1) + load_planes("xo", xo, 1, 1)
        w2_raw = load_words(nc.sync, "w2_raw", w2_words)
        w_raw = load_words(nc.sync, "w_raw", w_words)
        w2s_raw = load_scales(nc.gpsimd, "w2s_raw", w2_scales)
        xo_win = xo_win + load_planes("xo", xo, 2, 1) + load_planes("xo", xo, 3, 1)
        ws_raw = load_scales(nc.vector, "ws_raw", w_scales)
        xa_win = load_planes("xa", xa, 0, 2)
        nc.sync.dma_start(list_a[:], offs)
        xa_win = xa_win + load_planes("xa", xa, 2, 2)
        nc.sync.dma_start(list_b[:], offs2)
        xb_win = load_planes("xb", xb, 0, 2) + load_planes("xb", xb, 2, 1) + load_planes("xb", xb, 3, 1)
        wb_sb = load_words(nc.sync, "wb_sb", wb_words)
        wbs_sb = load_scales(nc.vector, "wbs_sb", wb_scales)
        rs_sb = sb("rs_sb", [P, 2, N], F32)
        nc.sync.dma_start(out=rs_sb[:], in_=rs.rearrange("(h p) n -> p h n", h=2))

        neg_fl = sb("neg_fl", [P, PACK], F32)
        nc.scalar.activation(out=neg_fl[:], in_=fl_sb[:], func=ACT.Copy, scale=-1.0)

        def deal_words(copy, name, words):
            dealt = sb(name, [P, 2 * R], U8)
            copy(
                out=dealt[:].bitcast(U16).rearrange("p (t m) -> p t m", t=PACK),
                in_=words[:].bitcast(U16).rearrange("p (m t) -> p t m", t=PACK),
            )
            return dealt

        def deal_scales(name, scales):
            dealt = sb(name, [P, R], U8)
            nc.vector.tensor_copy(
                out=dealt[:].rearrange("p (t m) -> p t m", t=PACK), in_=scales.rearrange("p (m t) -> p t m", t=PACK)
            )
            return dealt


        def quantize(name, grouped, cols, fmt, codes_name=None):
            codes = sb(codes_name or name + "_codes", [P, cols], U32)
            scales = sb(name + "_scales", [P, cols], U8)
            nc.vector.quantize_mx(
                out=codes[:].bitcast(fmt), scales=scales[:], in_=grouped[:].rearrange("p j t -> p (j t)")
            )
            return codes, scales

        u2 = sb("u2", [P, J, PACK], BF16)

        def side_plane(t):
            picked = sb("picked%d" % t, [P, J], F32)
            nc.scalar.activation(out=picked[:], in_=xo_win[t].indirect(list_o[:]), func=ACT.Copy)
            larger = sb("larger%d" % t, [P, J], F32)
            nc.vector.tensor_tensor(out=larger[:], in0=picked[:], in1=so_win[t], op=ALU.max)
            nc.vector.tensor_scalar(
                out=u2[:, :, t], in0=larger[:], scalar1=neg_fl[:, t : t + 1], scalar2=None, op0=ALU.mult
            )

        side_plane(0)
        side_plane(1)
        w_d = deal_words(nc.scalar.copy, "w_d", w_raw)
        w2_d = deal_words(nc.scalar.copy, "w2_d", w2_raw)
        w2s_d = deal_scales("w2s_d", w2s_raw)
        side_plane(2)
        side_plane(3)
        u2_codes, u2_scales = quantize("u2", u2, J, E5M2)
        ws_d = deal_scales("u2", ws_raw)

        gap = [psum.tile([P, PACK * H], F32, name="gap%d" % h) for h in range(2)]
        prod = [psum.tile([P, N], F32, name="prod%d" % h) for h in range(2)]

        def first_stage(h, words, scales, codes, code_scales, fmt, start, stop):
            for t in range(PACK):
                nc.tensor.matmul_mx(
                    out=gap[h][:, t * H : (t + 1) * H],
                    lhsT=words[:, 2 * t * P : 2 * (t + 1) * P].bitcast(E2M1),
                    lhsT_scale=scales[:, t * P : (t + 1) * P],
                    rhs=codes.bitcast(fmt),
                    rhs_scale=code_scales,
                    start=start and t == 0,
                    stop=stop and t == PACK - 1,
                )

        for h in range(2):
            cols = slice(h * H, (h + 1) * H)
            first_stage(h, w2_d, w2s_d, u2_codes[:, cols], u2_scales[:, cols], E5M2, True, False)

        def pick_planes(name, windows, lst):
            planes = sb(name, [P, len(windows), H], F32)
            for t, window in enumerate(windows):
                nc.scalar.activation(out=planes[:, t, :], in_=window.indirect(lst[:]), func=ACT.Copy)
            return planes[:].rearrange("p t j -> p j t")

        def close_gap(h, hid_name, codes, scales):
            first_stage(h, w_d, ws_d, codes[:], scales[:], E4M3, False, True)
            hid = sb(hid_name, [P, H, PACK], BF16)
            nc.scalar.activation(out=hid[:], in_=gap[h][:].rearrange("p (t j) -> p j t", t=PACK), func=ACT.Abs)
            return hid

        def second_stage(h, codes, scales):
            nc.tensor.matmul_mx(
                out=prod[h][:],
                lhsT=codes[:].bitcast(E5M2),
                lhsT_scale=scales[:],
                rhs=wb_sb[:].bitcast(E2M1),
                rhs_scale=wbs_sb,
                start=True,
                stop=True,
            )

        def row_factor(h):
            size = sb("size%d" % h, [P, N], F32)
            nc.scalar.activation(out=size[:], in_=prod[h][:], func=ACT.Abs)
            lifted = sb("lifted%d" % h, [P, N], F32)
            peak = sb("peak%d" % h, [P, 1], F32)
            nc.vector.tensor_scalar(
                out=lifted[:], in0=size[:], scalar1=0.2, scalar2=None, op0=ALU.add, op1=ALU.max, accum_out=peak[:]
            )
            inverse = sb("inverse%d" % h, [P, 1], F32)
            nc.vector.reciprocal(out=inverse[:], in_=peak[:])
            return inverse

        def finish(h, name, inverse, rs_part):
            result = sb(name, [P, N], F32)
            nc.vector.scalar_tensor_tensor(
                out=result[:], in0=prod[h][:], scalar=inverse[:], in1=rs_part[:, h, :], op0=ALU.mult, op1=ALU.add
            )
            nc.sync.dma_start(out=out[h * H : (h + 1) * H, :], in_=result[:])

        u0 = sb("u0", [P, H, PACK], BF16)
        nc.vector.tensor_copy(out=u0[:], in_=pick_planes("xa_picked", xa_win, list_a))
        xb_picked = pick_planes("xb_picked", xb_win[0:2], list_b)
        u0_quantized = quantize("u0", u0, H, E4M3)
        u1 = sb("u1", [P, H, PACK], BF16)
        nc.scalar.copy(out=u1[:, :, 0:2], in_=xb_picked)
        hid0 = close_gap(0, "xb_picked", *u0_quantized)
        for t in range(2, PACK):
            nc.vector.tensor_copy(out=u1[:, :, t], in_=xb_win[t].indirect(list_b[:]))
        hid1 = close_gap(1, "hid1", *quantize("u1", u1, H, E4M3))
        second_stage(0, *quantize("hid0", hid0, H, E5M2, "u1"))
        rs_part = sb("xb_picked", [P, 2, N], F32)
        nc.vector.tensor_scalar(out=rs_part[:], in0=rs_sb[:], scalar1=0.3, scalar2=None, op0=ALU.mult)
        second_stage(1, *quantize("hid1", hid1, H, E5M2))
        inverse0 = row_factor(0)
        inverse1 = row_factor(1)
        finish(0, "size1", inverse0, rs_part)
        finish(1, "result1", inverse1, rs_part)
